import numpy as np
import ml_dtypes


def mxq(x, axis, fmt="e4m3"):
    dtype, down = {"e4m3": (ml_dtypes.float8_e4m3fn, 7), "e5m2": (ml_dtypes.float8_e5m2, 14)}[fmt]
    v = np.moveaxis(np.asarray(x, np.float32).astype(ml_dtypes.bfloat16).astype(np.float64), axis, -1)
    blocks = v.reshape(v.shape[:-1] + (-1, 32))
    amax = np.abs(blocks).max(-1, keepdims=True)
    byte = np.maximum(np.where(amax > 0, np.frexp(amax)[1] - 1 + 127, 0) - down, 1)
    scale = np.exp2(byte - 127.0)
    codes = (blocks / scale).astype(np.float32).astype(dtype).astype(np.float64)
    return np.moveaxis((codes * scale).reshape(v.shape), -1, axis)


WIDE = False


def mx_kscale(k):
    if not WIDE:
        return np.ones(k)
    levels = np.array([10, -10, 5, -5, 0])
    if k % 512:
        return np.exp2(np.random.permutation(np.resize(levels, k // 32))).repeat(32)
    a = np.empty((k // 512, 16))
    for p in range(k // 512):
        a[p, :8] = np.random.permutation(np.resize(levels, 8))
        for g in range(8):
            far = levels[np.abs(levels - a[p, g]) >= 10]
            a[p, g + 8] = far[np.random.randint(len(far))]
    return np.exp2(a.ravel()).repeat(32)


def f64(x):
    return np.asarray(x).astype(np.float64)


def striped(idx):
    return np.tile(idx.reshape(-1, 16).T, (8, 1)).astype(np.uint16)


def unstriped(offs):
    return offs[:16].T.reshape(-1).astype(np.int64)


def pack_weight(w):
    k, n = w.shape
    w = f64(np.asarray(w, np.float32).astype(ml_dtypes.bfloat16)).reshape(k // 32, 32, n)
    amax = np.abs(w).max(1)
    byte = np.clip(np.where(amax > 0, np.frexp(amax)[1] - 1 + 127 - 7, 1), 1, 254)
    scaled = (w * np.exp2(127.0 - byte)[:, None, :]).reshape(k, n).astype(np.float32)
    words = np.ascontiguousarray(scaled.reshape(k // 512, 128, 4, n).transpose(0, 1, 3, 2)).astype(ml_dtypes.float8_e4m3fn).view(np.uint8)
    return words, np.ascontiguousarray(byte.astype(np.uint8).reshape(k // 512, 16, n))


def unpack_weight(words, scales):
    g, p, n, _ = words.shape
    vals = np.ascontiguousarray(words).view(ml_dtypes.float8_e4m3fn).astype(np.float64) * np.repeat(np.exp2(scales.astype(np.float64) - 127.0), 8, axis=1)[..., None]
    return vals.transpose(0, 1, 3, 2).reshape(g * 512, n)


def gelu(v):
    return 0.5 * v * (1.0 + np.tanh(np.sqrt(2.0 / np.pi) * (v + 0.044715 * v**3)))


K, T, E, C, N = 2048, 512, 8, 128, 256


def by_expert(wq, xq):
    return np.concatenate([wq[e].T @ xq[:, e * C:(e + 1) * C] for e in range(E)], axis=1)


def setup_inputs():
    n = np.random.standard_normal
    s = mx_kscale(K)[:, None]
    first = np.random.permutation(np.repeat(np.arange(E), T // E))
    second = (first + 1 + np.random.permutation(np.repeat(np.arange(E - 1), -(-T // (E - 1)))[:T])) % E
    while np.bincount(second, minlength=E).max() != T // E:
        load = np.bincount(second, minlength=E); hi, lo = int(load.argmax()), int(load.argmin())
        t = np.flatnonzero((second == hi) & (first != lo))[0]; second[t] = lo
    slot_token = np.empty(E * C, np.int64); pos = np.empty((2, T), np.int64); fill = np.zeros(E, np.int64)
    place = np.stack([np.random.permutation(C) for _ in range(E)])
    for r, deal in enumerate((first, second)):
        for t in np.random.permutation(T):
            e = deal[t]; j = e * C + place[e, fill[e]]; fill[e] += 1; slot_token[j] = t; pos[r, t] = j
    g = np.random.uniform(0.2, 0.8, T)
    packed = [pack_weight(m) for m in n((E, K, N)) / np.sqrt(K) / s[None]]
    return {
        "xT": (n((K, T)) * s).astype(np.float32),
        "w_words": np.stack([m[0] for m in packed]),
        "w_scales": np.stack([m[1] for m in packed]),
        "b": (0.3 * n((N, E))).astype(np.float32),
        "gate": np.stack([np.tile(g, (N, 1)), np.tile(1.0 - g, (N, 1))]).astype(np.float32),
        "offs": striped(slot_token),
        "pos1": striped(pos[0]),
        "pos2": striped(pos[1]),
    }


def reference(xT, w_words, w_scales, b, gate, offs, pos1, pos2):
    idx = unstriped(offs)
    xq = mxq(f64(xT)[:, idx], 0, "e4m3")
    w = np.stack([unpack_weight(w_words[e], w_scales[e]) for e in range(E)])
    y = by_expert(w, xq)
    y = gelu(y + np.repeat(f64(b), C, axis=1))
    return f64(gate[0]) * y[:, unstriped(pos1)] + f64(gate[1]) * y[:, unstriped(pos2)]

@@ -1,0 +1,179 @@
+from contextlib import ExitStack
+
+import concourse.mybir as mybir
+
+K, T, E, C, N = 2048, 512, 8, 128, 256
+SLOTS = E * C
+P = 128
+PACK = 4
+K_PASS = P * PACK
+PASSES = K // K_PASS
+M = 128
+HALVES = N // M
+
+FLOPS = 2 * SLOTS * K * N
+
+F32 = mybir.dt.float32
+BF16 = mybir.dt.bfloat16
+I32 = mybir.dt.int32
+U32 = mybir.dt.uint32
+U16 = mybir.dt.uint16
+U8 = mybir.dt.uint8
+FP8X4 = mybir.dt.float8_e4m3fn_x4
+GELU = mybir.ActivationFunctionType.Gelu_apprx_tanh
+MULT = mybir.AluOpType.mult
+ADD = mybir.AluOpType.add
+
+CUTS = [(0, 384), (384, 768), (768, 1024)]
+SCALAR_TOKENS = (0, 288, 416, 512)
+
+
+def tile_routed_moe_kernel(tc, xT, w_words, w_scales, b, gate, offs, pos1, pos2, out):
+    nc = tc.nc
+    with ExitStack() as ctx:
+        keep = ctx.enter_context(tc.tile_pool(name="keep", bufs=1))
+        psum = ctx.enter_context(tc.psum_pool(name="psum", bufs=8))
+
+        offs_sb = keep.tile([P, SLOTS // 16], U16, name="offs_sb")
+        pos1_sb = keep.tile([P, T // 16], U16, name="pos1_sb")
+        pos2_sb = keep.tile([P, T // 16], U16, name="pos2_sb")
+        bias = keep.tile([P, HALVES, E], F32, name="bias")
+        w_sc = keep.tile([P, E * PASSES, N], U8, name="w_sc", align_bytes=64)
+        t_sc = keep.tile([P, T], U8, name="t_sc", align_bytes=64)
+        g_sc = keep.tile([P, SLOTS], U8, name="g_sc", align_bytes=64)
+
+        nc.gpsimd.memset(t_sc[:], 0)
+        nc.gpsimd.memset(w_sc[:].rearrange("p a n -> p (a n)").bitcast(I32), 0)
+        warm = keep.tile([P, 1], F32, name="warm")
+        nc.vector.memset(warm[:], 0.0)
+        warm_out = keep.tile([P, 1], F32, name="warm_out")
+        nc.scalar.activation(warm_out[:], warm[:], GELU)
+
+        raw = []
+        xb = []
+        t_w = []
+        g_w = []
+        w_w = []
+        for a in range(PASSES):
+            raw.append(keep.tile([P, PACK, T], F32, name="raw%d" % a))
+            xb.append(keep.tile([P, T, PACK], BF16, name="xb%d" % a, align_bytes=64))
+            t_w.append(keep.tile([P, T], U32, name="t_w%d" % a, align_bytes=64))
+            g_w.append(keep.tile([P, SLOTS], U32, name="g_w%d" % a, align_bytes=64))
+        for e2 in range(E // 2 - 1):
+            w_w.append(keep.tile([P, 2 * PASSES, N], U32, name="w_w%d" % e2, align_bytes=64))
+        w_last = [keep.tile([P, 2 * PASSES, M], U32, name="w_last%d" % h, align_bytes=64) for h in range(HALVES)]
+        gates = [keep.tile([P, 2, T], F32, name="gate%d" % h) for h in range(HALVES)]
+        y = [keep.tile([P, SLOTS], F32, name="y%d" % h) for h in range(HALVES)]
+
+        def load_x(a, t0, t1):
+            nc.sync.dma_start(
+                raw[a][:, :, t0:t1],
+                xT[a * K_PASS : (a + 1) * K_PASS, t0:t1].rearrange("(p j) w -> p j w", j=PACK),
+            )
+
+        def load_w_scales(q):
+            nc.sync.dma_start(
+                w_sc[32 * q : 32 * q + 4, :, :].bitcast(I32),
+                w_scales[:, :, 4 * q : 4 * q + 4, :].rearrange("e a q n -> q (e a) n").bitcast(I32),
+            )
+
+        def load_w(dst, e2, n0, n1):
+            nc.sync.dma_start(
+                dst[:].bitcast(I32),
+                w_words[2 * e2 : 2 * e2 + 2].rearrange("e a p n r -> p (e a) (n r)")[:, :, n0 * PACK : n1 * PACK].bitcast(I32),
+            )
+
+        def load_gate(h):
+            nc.sync.dma_start(gates[h][:], gate[:, h * M : (h + 1) * M, :].rearrange("g p t -> p g t"))
+
+        load_x(0, 0, 256)
+        load_x(0, 256, 512)
+        nc.sync.dma_start(offs_sb[:], offs)
+        load_x(1, 0, 512)
+        load_x(2, 0, 512)
+        load_w_scales(0)
+        load_w_scales(1)
+        load_x(3, 0, 512)
+        load_w_scales(2)
+        load_w_scales(3)
+        load_w(w_w[0], 0, 0, N)
+        nc.sync.dma_start(bias[:], b.rearrange("(h p) e -> p h e", p=M))
+        load_w(w_w[1], 1, 0, N)
+        nc.sync.dma_start(pos1_sb[:], pos1)
+        load_w(w_w[2], 2, 0, N)
+        nc.sync.dma_start(pos2_sb[:], pos2)
+        load_gate(0)
+        load_w(w_last[0], 3, 0, M)
+        load_gate(1)
+        load_w(w_last[1], 3, M, N)
+
+        def cast(engine_copy, a, t0, t1):
+            engine_copy(
+                xb[a][:, t0:t1, :].rearrange("p (c i) j -> p c j i", i=4),
+                raw[a][:, :, t0:t1].rearrange("p j (c i) -> p c j i", i=4),
+            )
+
+        def quantize(a, t0, t1):
+            nc.vector.quantize_mx(
+                out=t_w[a][:, t0:t1].bitcast(FP8X4),
+                scales=t_sc[4 * a :, t0:t1],
+                in_=xb[a][:, t0:t1, :].rearrange("p w j -> p (w j)"),
+            )
+
+        def gather(dst, src, s0, s1):
+            nc.vector.tensor_copy(dst[:, s0:s1], src[:].indirect(offs_sb[:, s0 // 16 : s1 // 16]))
+
+        for a in range(PASSES):
+            if a == 0:
+                for t0 in (0, 256):
+                    cast(nc.scalar.copy, a, t0, t0 + 80)
+                    cast(nc.vector.tensor_copy, a, t0 + 80, t0 + 256)
+            else:
+                cast(nc.scalar.copy, a, 0, SCALAR_TOKENS[a])
+                if SCALAR_TOKENS[a] < T:
+                    cast(nc.vector.tensor_copy, a, SCALAR_TOKENS[a], T)
+            quantize(a, 0, T)
+            if a == PASSES - 1:
+                for s0, s1 in CUTS:
+                    gather(g_sc, t_sc, s0, s1)
+            for s0, s1 in CUTS:
+                gather(g_w[a], t_w[a], s0, s1)
+
+        def expert(e, h):
+            acc = psum.tile([M, 512], F32, name="acc")
+            cols = slice(e * C, (e + 1) * C)
+            n_cols = slice(h * M, (h + 1) * M)
+            if e < 6:
+                weights = w_w[e // 2][:, :, n_cols]
+            else:
+                weights = w_last[h]
+            for a in range(PASSES):
+                nc.tensor.matmul_mx(
+                    out=acc[:, :C],
+                    lhsT=weights[:, e % 2 * PASSES + a, :].bitcast(FP8X4),
+                    lhsT_scale=w_sc[:, e * PASSES + a, n_cols],
+                    rhs=g_w[a][:, cols].bitcast(FP8X4),
+                    rhs_scale=g_sc[4 * a :, cols],
+                    start=(a == 0),
+                    stop=(a == PASSES - 1),
+                )
+            nc.scalar.activation(y[h][:, cols], acc[:, :C], GELU, bias=bias[:, h, e : e + 1])
+
+        def combine(h):
+            one = keep.tile([P, T], F32, name="one%d" % h)
+            two = keep.tile([P, T], F32, name="two%d" % h)
+            both = keep.tile([P, T], F32, name="both%d" % h)
+            nc.vector.tensor_tensor(one[:], y[h][:].indirect(pos1_sb[:]), gates[h][:, 0, :], MULT)
+            nc.vector.tensor_tensor(two[:], y[h][:].indirect(pos2_sb[:]), gates[h][:, 1, :], MULT)
+            nc.vector.tensor_tensor(both[:], one[:], two[:], ADD)
+            nc.sync.dma_start(out[h * M : (h + 1) * M, :], both[:])
+
+        for e in range(6):
+            expert(e, 0)
+            expert(e, 1)
+        expert(6, 0)
+        expert(7, 0)
+        combine(0)
+        expert(6, 1)
+        expert(7, 1)
+        combine(1)

@@ -24,8 +24,13 @@ GELU = mybir.ActivationFunctionType.Gelu_apprx_tanh
 MULT = mybir.AluOpType.mult
 ADD = mybir.AluOpType.add
 
-CUTS = [(0, 384), (384, 768), (768, 1024)]
-SCALAR_TOKENS = (0, 288, 416, 512)
+CUTS = (
+    ((0, 384), (384, 768), (768, 1024)),
+    ((0, 768), (768, 1024)),
+    ((0, 1024),),
+    ((0, 512), (512, 1024)),
+)
+SCALAR_TOKENS = (0, 384, 512, 512)
 
 
 def tile_routed_moe_kernel(tc, xT, w_words, w_scales, b, gate, offs, pos1, pos2, out):
@@ -39,10 +44,11 @@ def tile_routed_moe_kernel(tc, xT, w_words, w_scales, b, gate, offs, pos1, pos2,
         pos2_sb = keep.tile([P, T // 16], U16, name="pos2_sb")
         bias = keep.tile([P, HALVES, E], F32, name="bias")
         w_sc = keep.tile([P, E * PASSES, N], U8, name="w_sc", align_bytes=64)
-        t_sc = keep.tile([P, T], U8, name="t_sc", align_bytes=64)
+        t_sc = keep.tile([P, PASSES * T], U8, name="t_sc", align_bytes=64)
         g_sc = keep.tile([P, SLOTS], U8, name="g_sc", align_bytes=64)
 
-        nc.gpsimd.memset(t_sc[:], 0)
+        nc.gpsimd.memset(t_sc[:].bitcast(I32), 0)
+        t_w = keep.tile([P, PASSES * T], U32, name="t_w", align_bytes=64)
         nc.gpsimd.memset(w_sc[:].rearrange("p a n -> p (a n)").bitcast(I32), 0)
         warm = keep.tile([P, 1], F32, name="warm")
         nc.vector.memset(warm[:], 0.0)
@@ -51,13 +57,11 @@ def tile_routed_moe_kernel(tc, xT, w_words, w_scales, b, gate, offs, pos1, pos2,
 
         raw = []
         xb = []
-        t_w = []
         g_w = []
         w_w = []
         for a in range(PASSES):
             raw.append(keep.tile([P, PACK, T], F32, name="raw%d" % a))
             xb.append(keep.tile([P, T, PACK], BF16, name="xb%d" % a, align_bytes=64))
-            t_w.append(keep.tile([P, T], U32, name="t_w%d" % a, align_bytes=64))
             g_w.append(keep.tile([P, SLOTS], U32, name="g_w%d" % a, align_bytes=64))
         for e2 in range(E // 2 - 1):
             w_w.append(keep.tile([P, 2 * PASSES, N], U32, name="w_w%d" % e2, align_bytes=64))
@@ -71,10 +75,10 @@ def tile_routed_moe_kernel(tc, xT, w_words, w_scales, b, gate, offs, pos1, pos2,
                 xT[a * K_PASS : (a + 1) * K_PASS, t0:t1].rearrange("(p j) w -> p j w", j=PACK),
             )
 
-        def load_w_scales(q):
+        def load_w_scales(i):
             nc.sync.dma_start(
-                w_sc[32 * q : 32 * q + 4, :, :].bitcast(I32),
-                w_scales[:, :, 4 * q : 4 * q + 4, :].rearrange("e a q n -> q (e a) n").bitcast(I32),
+                w_sc[i : P : 32, :, :].bitcast(I32),
+                w_scales[:, :, i : 16 : 4, :].rearrange("e a q n -> q (e a) n").bitcast(I32),
             )
 
         def load_w(dst, e2, n0, n1):
@@ -91,12 +95,12 @@ def tile_routed_moe_kernel(tc, xT, w_words, w_scales, b, gate, offs, pos1, pos2,
         nc.sync.dma_start(offs_sb[:], offs)
         load_x(1, 0, 512)
         load_x(2, 0, 512)
+        load_x(3, 0, 512)
+        load_w(w_w[0], 0, 0, N)
         load_w_scales(0)
         load_w_scales(1)
-        load_x(3, 0, 512)
         load_w_scales(2)
         load_w_scales(3)
-        load_w(w_w[0], 0, 0, N)
         nc.sync.dma_start(bias[:], b.rearrange("(h p) e -> p h e", p=M))
         load_w(w_w[1], 1, 0, N)
         nc.sync.dma_start(pos1_sb[:], pos1)
@@ -113,41 +117,43 @@ def tile_routed_moe_kernel(tc, xT, w_words, w_scales, b, gate, offs, pos1, pos2,
                 raw[a][:, :, t0:t1].rearrange("p j (c i) -> p c j i", i=4),
             )
 
+        def place(a):
+            return (PASSES - 1 - a) * T
+
         def quantize(a, t0, t1):
             nc.vector.quantize_mx(
-                out=t_w[a][:, t0:t1].bitcast(FP8X4),
+                out=t_w[:, place(a) + t0 : place(a) + t1].bitcast(FP8X4),
                 scales=t_sc[4 * a :, t0:t1],
                 in_=xb[a][:, t0:t1, :].rearrange("p w j -> p (w j)"),
             )
 
         def gather(dst, src, s0, s1):
-            nc.vector.tensor_copy(dst[:, s0:s1], src[:].indirect(offs_sb[:, s0 // 16 : s1 // 16]))
+            nc.vector.tensor_copy(dst[:, s0:s1], src.indirect(offs_sb[:, s0 // 16 : s1 // 16]))
 
         for a in range(PASSES):
             if a == 0:
                 for t0 in (0, 256):
                     cast(nc.scalar.copy, a, t0, t0 + 80)
                     cast(nc.vector.tensor_copy, a, t0 + 80, t0 + 256)
+                    quantize(a, t0, t0 + 256)
             else:
                 cast(nc.scalar.copy, a, 0, SCALAR_TOKENS[a])
                 if SCALAR_TOKENS[a] < T:
                     cast(nc.vector.tensor_copy, a, SCALAR_TOKENS[a], T)
-            quantize(a, 0, T)
+                quantize(a, 0, T)
             if a == PASSES - 1:
-                for s0, s1 in CUTS:
-                    gather(g_sc, t_sc, s0, s1)
-            for s0, s1 in CUTS:
-                gather(g_w[a], t_w[a], s0, s1)
+                gather(g_sc, t_sc[:], 0, SLOTS)
+            for s0, s1 in CUTS[a]:
+                gather(g_w[a], t_w[:, place(a) :], s0, s1)
 
-        def expert(e, h):
-            acc = psum.tile([M, 512], F32, name="acc")
+        def multiply(acc, e, h, passes):
             cols = slice(e * C, (e + 1) * C)
             n_cols = slice(h * M, (h + 1) * M)
             if e < 6:
                 weights = w_w[e // 2][:, :, n_cols]
             else:
                 weights = w_last[h]
-            for a in range(PASSES):
+            for a in passes:
                 nc.tensor.matmul_mx(
                     out=acc[:, :C],
                     lhsT=weights[:, e % 2 * PASSES + a, :].bitcast(FP8X4),
@@ -157,7 +163,9 @@ def tile_routed_moe_kernel(tc, xT, w_words, w_scales, b, gate, offs, pos1, pos2,
                     start=(a == 0),
                     stop=(a == PASSES - 1),
                 )
-            nc.scalar.activation(y[h][:, cols], acc[:, :C], GELU, bias=bias[:, h, e : e + 1])
+
+        def activate(acc, e, h):
+            nc.scalar.activation(y[h][:, e * C : (e + 1) * C], acc[:, :C], GELU, bias=bias[:, h, e : e + 1])
 
         def combine(h):
             one = keep.tile([P, T], F32, name="one%d" % h)
@@ -168,12 +176,17 @@ def tile_routed_moe_kernel(tc, xT, w_words, w_scales, b, gate, offs, pos1, pos2,
             nc.vector.tensor_tensor(both[:], one[:], two[:], ADD)
             nc.sync.dma_start(out[h * M : (h + 1) * M, :], both[:])
 
-        for e in range(6):
-            expert(e, 0)
-            expert(e, 1)
-        expert(6, 0)
-        expert(7, 0)
+        banks = []
+        for e in range(E):
+            acc = psum.tile([M, 512], F32, name="acc")
+            banks.append(acc)
+            multiply(acc, e, 0, range(PASSES - 1))
+        for e in range(E):
+            multiply(banks[e], e, 0, (PASSES - 1,))
+            activate(banks[e], e, 0)
         combine(0)
-        expert(6, 1)
-        expert(7, 1)
+        for e in range(E):
+            acc = psum.tile([M, 512], F32, name="acc")
+            multiply(acc, e, 1, range(PASSES))
+            activate(acc, e, 1)
         combine(1)

@@ -65,8 +65,14 @@ def tile_routed_moe_kernel(tc, xT, w_words, w_scales, b, gate, offs, pos1, pos2,
             g_w.append(keep.tile([P, SLOTS], U32, name="g_w%d" % a, align_bytes=64))
         for e2 in range(E // 2 - 1):
             w_w.append(keep.tile([P, 2 * PASSES, N], U32, name="w_w%d" % e2, align_bytes=64))
-        w_last = [keep.tile([P, 2 * PASSES, M], U32, name="w_last%d" % h, align_bytes=64) for h in range(HALVES)]
-        gates = [keep.tile([P, 2, T], F32, name="gate%d" % h) for h in range(HALVES)]
+        w_last = {}
+        for e in (6, 7):
+            for h in range(HALVES):
+                w_last[e, h] = keep.tile([P, PASSES, M], U32, name="w_last%d_%d" % (e, h), align_bytes=64)
+        gates = {}
+        for h in range(HALVES):
+            for r in range(2):
+                gates[r, h] = keep.tile([P, T], F32, name="gate%d_%d" % (r, h))
         y = [keep.tile([P, SLOTS], F32, name="y%d" % h) for h in range(HALVES)]
 
         def load_x(a, t0, t1):
@@ -81,14 +87,19 @@ def tile_routed_moe_kernel(tc, xT, w_words, w_scales, b, gate, offs, pos1, pos2,
                 w_scales[:, :, i : 16 : 4, :].rearrange("e a q n -> q (e a) n").bitcast(I32),
             )
 
-        def load_w(dst, e2, n0, n1):
+        def load_w(dst, e0, e1, n0, n1):
             nc.sync.dma_start(
                 dst[:].bitcast(I32),
-                w_words[2 * e2 : 2 * e2 + 2].rearrange("e a p n r -> p (e a) (n r)")[:, :, n0 * PACK : n1 * PACK].bitcast(I32),
+                w_words[e0:e1].rearrange("e a p n r -> p (e a) (n r)")[:, :, n0 * PACK : n1 * PACK].bitcast(I32),
             )
 
+        def load_w_last(h):
+            for e in (6, 7):
+                load_w(w_last[e, h], e, e + 1, h * M, (h + 1) * M)
+
         def load_gate(h):
-            nc.sync.dma_start(gates[h][:], gate[:, h * M : (h + 1) * M, :].rearrange("g p t -> p g t"))
+            for r in range(2):
+                nc.sync.dma_start(gates[r, h][:], gate[r, h * M : (h + 1) * M, :])
 
         load_x(0, 0, 256)
         load_x(0, 256, 512)
@@ -96,20 +107,20 @@ def tile_routed_moe_kernel(tc, xT, w_words, w_scales, b, gate, offs, pos1, pos2,
         load_x(1, 0, 512)
         load_x(2, 0, 512)
         load_x(3, 0, 512)
-        load_w(w_w[0], 0, 0, N)
+        load_w(w_w[0], 0, 2, 0, N)
         load_w_scales(0)
         load_w_scales(1)
         load_w_scales(2)
         load_w_scales(3)
         nc.sync.dma_start(bias[:], b.rearrange("(h p) e -> p h e", p=M))
-        load_w(w_w[1], 1, 0, N)
+        load_w(w_w[1], 2, 4, 0, N)
         nc.sync.dma_start(pos1_sb[:], pos1)
-        load_w(w_w[2], 2, 0, N)
+        load_w(w_w[2], 4, 6, 0, N)
         nc.sync.dma_start(pos2_sb[:], pos2)
+        load_w_last(0)
         load_gate(0)
-        load_w(w_last[0], 3, 0, M)
+        load_w_last(1)
         load_gate(1)
-        load_w(w_last[1], 3, M, N)
 
         def cast(engine_copy, a, t0, t1):
             engine_copy(
@@ -150,13 +161,13 @@ def tile_routed_moe_kernel(tc, xT, w_words, w_scales, b, gate, offs, pos1, pos2,
             cols = slice(e * C, (e + 1) * C)
             n_cols = slice(h * M, (h + 1) * M)
             if e < 6:
-                weights = w_w[e // 2][:, :, n_cols]
+                weights = w_w[e // 2][:, e % 2 * PASSES : e % 2 * PASSES + PASSES, n_cols]
             else:
-                weights = w_last[h]
+                weights = w_last[e, h]
             for a in passes:
                 nc.tensor.matmul_mx(
                     out=acc[:, :C],
-                    lhsT=weights[:, e % 2 * PASSES + a, :].bitcast(FP8X4),
+                    lhsT=weights[:, a, :].bitcast(FP8X4),
                     lhsT_scale=w_sc[:, e * PASSES + a, n_cols],
                     rhs=g_w[a][:, cols].bitcast(FP8X4),
                     rhs_scale=g_sc[4 * a :, cols],
@@ -167,26 +178,31 @@ def tile_routed_moe_kernel(tc, xT, w_words, w_scales, b, gate, offs, pos1, pos2,
         def activate(acc, e, h):
             nc.scalar.activation(y[h][:, e * C : (e + 1) * C], acc[:, :C], GELU, bias=bias[:, h, e : e + 1])
 
-        def combine(h):
+        def combine(h, cuts):
             one = keep.tile([P, T], F32, name="one%d" % h)
             two = keep.tile([P, T], F32, name="two%d" % h)
             both = keep.tile([P, T], F32, name="both%d" % h)
-            nc.vector.tensor_tensor(one[:], y[h][:].indirect(pos1_sb[:]), gates[h][:, 0, :], MULT)
-            nc.vector.tensor_tensor(two[:], y[h][:].indirect(pos2_sb[:]), gates[h][:, 1, :], MULT)
-            nc.vector.tensor_tensor(both[:], one[:], two[:], ADD)
-            nc.sync.dma_start(out[h * M : (h + 1) * M, :], both[:])
+            nc.vector.tensor_tensor(one[:], y[h][:].indirect(pos1_sb[:]), gates[0, h][:], MULT)
+            nc.vector.tensor_tensor(two[:], y[h][:].indirect(pos2_sb[:]), gates[1, h][:], MULT)
+            for t0, t1 in cuts:
+                nc.vector.tensor_tensor(both[:, t0:t1], one[:, t0:t1], two[:, t0:t1], ADD)
+                nc.sync.dma_start(out[h * M : (h + 1) * M, t0:t1], both[:, t0:t1])
 
         banks = []
-        for e in range(E):
+        for e in range(6):
             acc = psum.tile([M, 512], F32, name="acc")
             banks.append(acc)
             multiply(acc, e, 0, range(PASSES - 1))
-        for e in range(E):
+        for e in range(6):
             multiply(banks[e], e, 0, (PASSES - 1,))
             activate(banks[e], e, 0)
-        combine(0)
+        for e in (6, 7):
+            acc = psum.tile([M, 512], F32, name="acc")
+            multiply(acc, e, 0, range(PASSES))
+            activate(acc, e, 0)
+        combine(0, ((0, T),))
         for e in range(E):
             acc = psum.tile([M, 512], F32, name="acc")
             multiply(acc, e, 1, range(PASSES))
             activate(acc, e, 1)
-        combine(1)
+        combine(1, ((0, 256), (256, T)))

@@ -11,6 +11,8 @@ PASSES = K // K_PASS
 M = 128
 HALVES = N // M
 
+PAD = 1024
+
 FLOPS = 2 * SLOTS * K * N
 
 F32 = mybir.dt.float32
@@ -25,11 +27,13 @@ MULT = mybir.AluOpType.mult
 ADD = mybir.AluOpType.add
 
 CUTS = (
-    ((0, 384), (384, 768), (768, 1024)),
-    ((0, 768), (768, 1024)),
+    ((0, 1024),),
+    ((0, 1024),),
     ((0, 1024),),
     ((0, 512), (512, 1024)),
 )
+FULL = 4
+HALF_LOADS = (((4, 6), (6, 8)), ((4, 6), (6, 8)))
 SCALAR_TOKENS = (0, 384, 512, 512)
 
 
@@ -45,10 +49,11 @@ def tile_routed_moe_kernel(tc, xT, w_words, w_scales, b, gate, offs, pos1, pos2,
         bias = keep.tile([P, HALVES, E], F32, name="bias")
         w_sc = keep.tile([P, E * PASSES, N], U8, name="w_sc", align_bytes=64)
         t_sc = keep.tile([P, PASSES * T], U8, name="t_sc", align_bytes=64)
-        g_sc = keep.tile([P, SLOTS], U8, name="g_sc", align_bytes=64)
+        g_sc = [keep.tile([P, 512], U8, name="g_sc%d" % i, align_bytes=64) for i in range(2)]
 
         nc.gpsimd.memset(t_sc[:].bitcast(I32), 0)
-        t_w = keep.tile([P, PASSES * T], U32, name="t_w", align_bytes=64)
+        t_w = keep.tile([P, PASSES * T + PAD], U32, name="t_w", align_bytes=64)
+        nc.gpsimd.memset(t_w[:, PASSES * T :].bitcast(I32), 0)
         nc.gpsimd.memset(w_sc[:].rearrange("p a n -> p (a n)").bitcast(I32), 0)
         warm = keep.tile([P, 1], F32, name="warm")
         nc.vector.memset(warm[:], 0.0)
@@ -58,21 +63,21 @@ def tile_routed_moe_kernel(tc, xT, w_words, w_scales, b, gate, offs, pos1, pos2,
         raw = []
         xb = []
         g_w = []
-        w_w = []
         for a in range(PASSES):
             raw.append(keep.tile([P, PACK, T], F32, name="raw%d" % a))
             xb.append(keep.tile([P, T, PACK], BF16, name="xb%d" % a, align_bytes=64))
-            g_w.append(keep.tile([P, SLOTS], U32, name="g_w%d" % a, align_bytes=64))
-        for e2 in range(E // 2 - 1):
-            w_w.append(keep.tile([P, 2 * PASSES, N], U32, name="w_w%d" % e2, align_bytes=64))
-        w_last = {}
-        for e in (6, 7):
-            for h in range(HALVES):
-                w_last[e, h] = keep.tile([P, PASSES, M], U32, name="w_last%d_%d" % (e, h), align_bytes=64)
-        gates = {}
+            g_w.append([keep.tile([P, 512], U32, name="g_w%d_%d" % (a, i), align_bytes=64) for i in range(2)] if a == 3 else [keep.tile([P, SLOTS], U32, name="g_w%d" % a, align_bytes=64)])
+        w_full = []
+        for i in range(FULL // 2):
+            w_full.append(keep.tile([P, 2 * PASSES, N], U32, name="w_full%d" % i, align_bytes=64))
+        w_half = {}
         for h in range(HALVES):
-            for r in range(2):
-                gates[r, h] = keep.tile([P, T], F32, name="gate%d_%d" % (r, h))
+            for e0, e1 in HALF_LOADS[h]:
+                tile = keep.tile([P, (e1 - e0) * PASSES, M], U32, name="w_half%d_%d" % (e0, h), align_bytes=64)
+                for e in range(e0, e1):
+                    w_half[e, h] = tile[:, (e - e0) * PASSES : (e - e0 + 1) * PASSES, :]
+                w_half[e0, e1, h] = tile
+        gates = [keep.tile([P, 2, T], F32, name="gate%d" % h) for h in range(HALVES)]
         y = [keep.tile([P, SLOTS], F32, name="y%d" % h) for h in range(HALVES)]
 
         def load_x(a, t0, t1):
@@ -93,13 +98,12 @@ def tile_routed_moe_kernel(tc, xT, w_words, w_scales, b, gate, offs, pos1, pos2,
                 w_words[e0:e1].rearrange("e a p n r -> p (e a) (n r)")[:, :, n0 * PACK : n1 * PACK].bitcast(I32),
             )
 
-        def load_w_last(h):
-            for e in (6, 7):
-                load_w(w_last[e, h], e, e + 1, h * M, (h + 1) * M)
+        def load_w_halves(h):
+            for e0, e1 in HALF_LOADS[h]:
+                load_w(w_half[e0, e1, h], e0, e1, h * M, (h + 1) * M)
 
         def load_gate(h):
-            for r in range(2):
-                nc.sync.dma_start(gates[r, h][:], gate[r, h * M : (h + 1) * M, :])
+            nc.sync.dma_start(gates[h][:], gate[:, h * M : (h + 1) * M, :].rearrange("g p t -> p g t"))
 
         load_x(0, 0, 256)
         load_x(0, 256, 512)
@@ -107,19 +111,18 @@ def tile_routed_moe_kernel(tc, xT, w_words, w_scales, b, gate, offs, pos1, pos2,
         load_x(1, 0, 512)
         load_x(2, 0, 512)
         load_x(3, 0, 512)
-        load_w(w_w[0], 0, 2, 0, N)
+        load_w(w_full[0], 0, 2, 0, N)
         load_w_scales(0)
         load_w_scales(1)
         load_w_scales(2)
         load_w_scales(3)
         nc.sync.dma_start(bias[:], b.rearrange("(h p) e -> p h e", p=M))
-        load_w(w_w[1], 2, 4, 0, N)
+        load_w(w_full[1], 2, 4, 0, N)
+        load_w_halves(0)
         nc.sync.dma_start(pos1_sb[:], pos1)
-        load_w(w_w[2], 4, 6, 0, N)
         nc.sync.dma_start(pos2_sb[:], pos2)
-        load_w_last(0)
         load_gate(0)
-        load_w_last(1)
+        load_w_halves(1)
         load_gate(1)
 
         def cast(engine_copy, a, t0, t1):
@@ -139,7 +142,7 @@ def tile_routed_moe_kernel(tc, xT, w_words, w_scales, b, gate, offs, pos1, pos2,
             )
 
         def gather(dst, src, s0, s1):
-            nc.vector.tensor_copy(dst[:, s0:s1], src.indirect(offs_sb[:, s0 // 16 : s1 // 16]))
+            nc.vector.tensor_copy(dst[:], src.indirect(offs_sb[:, s0 // 16 : s1 // 16]))
 
         for a in range(PASSES):
             if a == 0:
@@ -150,27 +153,26 @@ def tile_routed_moe_kernel(tc, xT, w_words, w_scales, b, gate, offs, pos1, pos2,
             else:
                 cast(nc.scalar.copy, a, 0, SCALAR_TOKENS[a])
                 if SCALAR_TOKENS[a] < T:
-                    cast(nc.vector.tensor_copy, a, SCALAR_TOKENS[a], T)
+                    cast(nc.gpsimd.tensor_copy, a, SCALAR_TOKENS[a], T)
                 quantize(a, 0, T)
-            if a == PASSES - 1:
-                gather(g_sc, t_sc[:], 0, SLOTS)
-            for s0, s1 in CUTS[a]:
-                gather(g_w[a], t_w[:, place(a) :], s0, s1)
+            for i, (s0, s1) in enumerate(CUTS[a]):
+                if a == PASSES - 1:
+                    gather(g_sc[i], t_sc[:], s0, s1)
+                gather(g_w[a][i], t_w[:, place(a) :], s0, s1)
 
         def multiply(acc, e, h, passes):
-            cols = slice(e * C, (e + 1) * C)
             n_cols = slice(h * M, (h + 1) * M)
-            if e < 6:
-                weights = w_w[e // 2][:, e % 2 * PASSES : e % 2 * PASSES + PASSES, n_cols]
+            if e < FULL:
+                weights = w_full[e // 2][:, e % 2 * PASSES : (e % 2 + 1) * PASSES, n_cols]
             else:
-                weights = w_last[e, h]
+                weights = w_half[e, h]
             for a in passes:
                 nc.tensor.matmul_mx(
                     out=acc[:, :C],
                     lhsT=weights[:, a, :].bitcast(FP8X4),
                     lhsT_scale=w_sc[:, e * PASSES + a, n_cols],
-                    rhs=g_w[a][:, cols].bitcast(FP8X4),
-                    rhs_scale=g_sc[4 * a :, cols],
+                    rhs=(g_w[a][e // 4][:, e % 4 * C : (e % 4 + 1) * C] if a == 3 else g_w[a][0][:, e * C : (e + 1) * C]).bitcast(FP8X4),
+                    rhs_scale=g_sc[e // 4][4 * a :, e % 4 * C : (e % 4 + 1) * C],
                     start=(a == 0),
                     stop=(a == PASSES - 1),
                 )
@@ -182,24 +184,21 @@ def tile_routed_moe_kernel(tc, xT, w_words, w_scales, b, gate, offs, pos1, pos2,
             one = keep.tile([P, T], F32, name="one%d" % h)
             two = keep.tile([P, T], F32, name="two%d" % h)
             both = keep.tile([P, T], F32, name="both%d" % h)
-            nc.vector.tensor_tensor(one[:], y[h][:].indirect(pos1_sb[:]), gates[0, h][:], MULT)
-            nc.vector.tensor_tensor(two[:], y[h][:].indirect(pos2_sb[:]), gates[1, h][:], MULT)
+            nc.vector.tensor_tensor(one[:], y[h][:].indirect(pos1_sb[:]), gates[h][:, 0, :], MULT)
+            nc.vector.tensor_tensor(two[:], y[h][:].indirect(pos2_sb[:]), gates[h][:, 1, :], MULT)
             for t0, t1 in cuts:
                 nc.vector.tensor_tensor(both[:, t0:t1], one[:, t0:t1], two[:, t0:t1], ADD)
                 nc.sync.dma_start(out[h * M : (h + 1) * M, t0:t1], both[:, t0:t1])
 
         banks = []
-        for e in range(6):
-            acc = psum.tile([M, 512], F32, name="acc")
-            banks.append(acc)
-            multiply(acc, e, 0, range(PASSES - 1))
-        for e in range(6):
-            multiply(banks[e], e, 0, (PASSES - 1,))
-            activate(banks[e], e, 0)
-        for e in (6, 7):
-            acc = psum.tile([M, 512], F32, name="acc")
-            multiply(acc, e, 0, range(PASSES))
-            activate(acc, e, 0)
+        for e0 in (0, 4):
+            for e in range(e0, e0 + 4):
+                acc = psum.tile([M, 512], F32, name="acc")
+                banks.append(acc)
+                multiply(acc, e, 0, range(PASSES - 1))
+            for e in range(e0, e0 + 4):
+                multiply(banks[e], e, 0, (PASSES - 1,))
+                activate(banks[e], e, 0)
         combine(0, ((0, T),))
         for e in range(E):
             acc = psum.tile([M, 512], F32, name="acc")

from contextlib import ExitStack

import concourse.mybir as mybir

K, T, E, C, N = 2048, 512, 8, 128, 256
SLOTS = E * C
P = 128
PACK = 4
K_PASS = P * PACK
PASSES = K // K_PASS
M = 128
HALVES = N // M

PAD = 1024

FLOPS = 2 * SLOTS * K * N

F32 = mybir.dt.float32
BF16 = mybir.dt.bfloat16
I32 = mybir.dt.int32
U32 = mybir.dt.uint32
U16 = mybir.dt.uint16
U8 = mybir.dt.uint8
FP8X4 = mybir.dt.float8_e4m3fn_x4
GELU = mybir.ActivationFunctionType.Gelu_apprx_tanh
MULT = mybir.AluOpType.mult
ADD = mybir.AluOpType.add

CUTS = (
    ((0, 1024),),
    ((0, 1024),),
    ((0, 1024),),
    ((0, 512), (512, 1024)),
)
FULL = 4
HALF_LOADS = (((4, 6), (6, 8)), ((4, 6), (6, 8)))
SCALAR_TOKENS = (0, 384, 512, 512)


def tile_routed_moe_kernel(tc, xT, w_words, w_scales, b, gate, offs, pos1, pos2, out):
    nc = tc.nc
    with ExitStack() as ctx:
        keep = ctx.enter_context(tc.tile_pool(name="keep", bufs=1))
        psum = ctx.enter_context(tc.psum_pool(name="psum", bufs=8))

        offs_sb = keep.tile([P, SLOTS // 16], U16, name="offs_sb")
        pos1_sb = keep.tile([P, T // 16], U16, name="pos1_sb")
        pos2_sb = keep.tile([P, T // 16], U16, name="pos2_sb")
        bias = keep.tile([P, HALVES, E], F32, name="bias")
        w_sc = keep.tile([P, E * PASSES, N], U8, name="w_sc", align_bytes=64)
        t_sc = keep.tile([P, PASSES * T], U8, name="t_sc", align_bytes=64)
        g_sc = [keep.tile([P, 512], U8, name="g_sc%d" % i, align_bytes=64) for i in range(2)]

        nc.gpsimd.memset(t_sc[:].bitcast(I32), 0)
        t_w = keep.tile([P, PASSES * T + PAD], U32, name="t_w", align_bytes=64)
        nc.gpsimd.memset(t_w[:, PASSES * T :].bitcast(I32), 0)
        nc.gpsimd.memset(w_sc[:].rearrange("p a n -> p (a n)").bitcast(I32), 0)
        warm = keep.tile([P, 1], F32, name="warm")
        nc.vector.memset(warm[:], 0.0)
        warm_out = keep.tile([P, 1], F32, name="warm_out")
        nc.scalar.activation(warm_out[:], warm[:], GELU)

        raw = []
        xb = []
        g_w = []
        for a in range(PASSES):
            raw.append(keep.tile([P, PACK, T], F32, name="raw%d" % a))
            xb.append(keep.tile([P, T, PACK], BF16, name="xb%d" % a, align_bytes=64))
            g_w.append([keep.tile([P, 512], U32, name="g_w%d_%d" % (a, i), align_bytes=64) for i in range(2)] if a == 3 else [keep.tile([P, SLOTS], U32, name="g_w%d" % a, align_bytes=64)])
        w_full = []
        for i in range(FULL // 2):
            w_full.append(keep.tile([P, 2 * PASSES, N], U32, name="w_full%d" % i, align_bytes=64))
        w_half = {}
        for h in range(HALVES):
            for e0, e1 in HALF_LOADS[h]:
                tile = keep.tile([P, (e1 - e0) * PASSES, M], U32, name="w_half%d_%d" % (e0, h), align_bytes=64)
                for e in range(e0, e1):
                    w_half[e, h] = tile[:, (e - e0) * PASSES : (e - e0 + 1) * PASSES, :]
                w_half[e0, e1, h] = tile
        gates = [keep.tile([P, 2, T], F32, name="gate%d" % h) for h in range(HALVES)]
        y = [keep.tile([P, SLOTS], F32, name="y%d" % h) for h in range(HALVES)]

        def load_x(a, t0, t1):
            nc.sync.dma_start(
                raw[a][:, :, t0:t1],
                xT[a * K_PASS : (a + 1) * K_PASS, t0:t1].rearrange("(p j) w -> p j w", j=PACK),
            )

        def load_w_scales(i):
            nc.sync.dma_start(
                w_sc[i : P : 32, :, :].bitcast(I32),
                w_scales[:, :, i : 16 : 4, :].rearrange("e a q n -> q (e a) n").bitcast(I32),
            )

        def load_w(dst, e0, e1, n0, n1):
            nc.sync.dma_start(
                dst[:].bitcast(I32),
                w_words[e0:e1].rearrange("e a p n r -> p (e a) (n r)")[:, :, n0 * PACK : n1 * PACK].bitcast(I32),
            )

        def load_w_halves(h):
            for e0, e1 in HALF_LOADS[h]:
                load_w(w_half[e0, e1, h], e0, e1, h * M, (h + 1) * M)

        def load_gate(h):
            nc.sync.dma_start(gates[h][:], gate[:, h * M : (h + 1) * M, :].rearrange("g p t -> p g t"))

        load_x(0, 0, 256)
        load_x(0, 256, 512)
        nc.sync.dma_start(offs_sb[:], offs)
        load_x(1, 0, 512)
        load_x(2, 0, 512)
        load_x(3, 0, 512)
        load_w(w_full[0], 0, 2, 0, N)
        load_w_scales(0)
        load_w_scales(1)
        load_w_scales(2)
        load_w_scales(3)
        nc.sync.dma_start(bias[:], b.rearrange("(h p) e -> p h e", p=M))
        load_w(w_full[1], 2, 4, 0, N)
        load_w_halves(0)
        nc.sync.dma_start(pos1_sb[:], pos1)
        nc.sync.dma_start(pos2_sb[:], pos2)
        load_gate(0)
        load_w_halves(1)
        load_gate(1)

        def cast(engine_copy, a, t0, t1):
            engine_copy(
                xb[a][:, t0:t1, :].rearrange("p (c i) j -> p c j i", i=4),
                raw[a][:, :, t0:t1].rearrange("p j (c i) -> p c j i", i=4),
            )

        def place(a):
            return (PASSES - 1 - a) * T

        def quantize(a, t0, t1):
            nc.vector.quantize_mx(
                out=t_w[:, place(a) + t0 : place(a) + t1].bitcast(FP8X4),
                scales=t_sc[4 * a :, t0:t1],
                in_=xb[a][:, t0:t1, :].rearrange("p w j -> p (w j)"),
            )

        def gather(dst, src, s0, s1):
            nc.vector.tensor_copy(dst[:], src.indirect(offs_sb[:, s0 // 16 : s1 // 16]))

        for a in range(PASSES):
            if a == 0:
                for t0 in (0, 256):
                    cast(nc.scalar.copy, a, t0, t0 + 80)
                    cast(nc.vector.tensor_copy, a, t0 + 80, t0 + 256)
                    quantize(a, t0, t0 + 256)
            else:
                cast(nc.scalar.copy, a, 0, SCALAR_TOKENS[a])
                if SCALAR_TOKENS[a] < T:
                    cast(nc.gpsimd.tensor_copy, a, SCALAR_TOKENS[a], T)
                quantize(a, 0, T)
            for i, (s0, s1) in enumerate(CUTS[a]):
                if a == PASSES - 1:
                    gather(g_sc[i], t_sc[:], s0, s1)
                gather(g_w[a][i], t_w[:, place(a) :], s0, s1)

        def multiply(acc, e, h, passes):
            n_cols = slice(h * M, (h + 1) * M)
            if e < FULL:
                weights = w_full[e // 2][:, e % 2 * PASSES : (e % 2 + 1) * PASSES, n_cols]
            else:
                weights = w_half[e, h]
            for a in passes:
                nc.tensor.matmul_mx(
                    out=acc[:, :C],
                    lhsT=weights[:, a, :].bitcast(FP8X4),
                    lhsT_scale=w_sc[:, e * PASSES + a, n_cols],
                    rhs=(g_w[a][e // 4][:, e % 4 * C : (e % 4 + 1) * C] if a == 3 else g_w[a][0][:, e * C : (e + 1) * C]).bitcast(FP8X4),
                    rhs_scale=g_sc[e // 4][4 * a :, e % 4 * C : (e % 4 + 1) * C],
                    start=(a == 0),
                    stop=(a == PASSES - 1),
                )

        def activate(acc, e, h):
            nc.scalar.activation(y[h][:, e * C : (e + 1) * C], acc[:, :C], GELU, bias=bias[:, h, e : e + 1])

        def combine(h, cuts):
            one = keep.tile([P, T], F32, name="one%d" % h)
            two = keep.tile([P, T], F32, name="two%d" % h)
            both = keep.tile([P, T], F32, name="both%d" % h)
            nc.vector.tensor_tensor(one[:], y[h][:].indirect(pos1_sb[:]), gates[h][:, 0, :], MULT)
            nc.vector.tensor_tensor(two[:], y[h][:].indirect(pos2_sb[:]), gates[h][:, 1, :], MULT)
            for t0, t1 in cuts:
                nc.vector.tensor_tensor(both[:, t0:t1], one[:, t0:t1], two[:, t0:t1], ADD)
                nc.sync.dma_start(out[h * M : (h + 1) * M, t0:t1], both[:, t0:t1])

        banks = []
        for e0 in (0, 4):
            for e in range(e0, e0 + 4):
                acc = psum.tile([M, 512], F32, name="acc")
                banks.append(acc)
                multiply(acc, e, 0, range(PASSES - 1))
            for e in range(e0, e0 + 4):
                multiply(banks[e], e, 0, (PASSES - 1,))
                activate(banks[e], e, 0)
        combine(0, ((0, T),))
        for e in range(E):
            acc = psum.tile([M, 512], F32, name="acc")
            multiply(acc, e, 1, range(PASSES))
            activate(acc, e, 1)
        combine(1, ((0, 256), (256, T)))
